import numpy as np
import ml_dtypes

BF16 = ml_dtypes.bfloat16


def bf(x):
    return np.asarray(x, np.float32).astype(BF16)


def f32(x):
    return np.asarray(x, np.float32)


def f64(x):
    return np.asarray(x).astype(np.float64)


def striped(idx):
    return np.tile(idx.reshape(-1, 16).T, (8, 1))


S, K, M, N, D, V = 4096, 256, 256, 1024, 8, 128


def sigmoid(v):
    return 1.0 / (1.0 + np.exp(-v))


def setup_inputs():
    return {"table": bf(np.random.standard_normal((K, S))), "w": bf(np.random.standard_normal((K, M)) / np.sqrt(K)), "b": f32(0.5 * np.random.standard_normal((M, 1))), "offs": striped(np.random.permutation(np.tile(np.arange(S), 2))[:N])}


def reference(table, w, b, offs):
    idx = offs[:16].T.reshape(-1)
    x = f64(table)[:, idx]
    y = f64(w).T @ x
    z = (y + f64(b)) * sigmoid(y + f64(b))
    return z.reshape(M, V, D).mean(axis=2)

@@ -1,0 +1,63 @@
+import concourse.mybir as mybir
+
+BF16, F32, U16 = mybir.dt.bfloat16, mybir.dt.float32, mybir.dt.uint16
+SILU = mybir.ActivationFunctionType.Silu
+ADD, MULT = mybir.AluOpType.add, mybir.AluOpType.mult
+AXIS_X = mybir.AxisListType.X
+
+P = 128
+S, K, M, N = 4096, 256, 256, 1024
+D = 8
+PIECE = 512
+KB, MB, PIECES = K // P, M // P, N // PIECE
+OFFS_COLS = PIECE // 16
+GROUPS = PIECE // D
+
+FLOPS = 2 * K * M * N
+
+
+def tile_gather_matmul_kernel(tc, table, w, b, offs, out):
+    nc = tc.nc
+    with (
+        tc.tile_pool(name="held", bufs=1) as held,
+        tc.psum_pool(name="psum", bufs=1) as psum,
+    ):
+        offsets = held.tile([P, N // 16], U16, name="offsets")
+        nc.sync.dma_start(offsets[:], offs)
+        weights = held.tile([P, KB, M], BF16, name="weights")
+        nc.scalar.dma_start(weights[:], w.rearrange("(a p) m -> p a m", p=P))
+        blocks = []
+        for k in range(KB):
+            block = held.tile([P, S], BF16, name=f"block{k}")
+            nc.sync.dma_start(block[:], table[k * P : (k + 1) * P, :])
+            blocks.append(block)
+        bias = held.tile([P, MB], F32, name="bias")
+        nc.scalar.dma_start(bias[:], b.rearrange("(a p) o -> p (a o)", p=P))
+
+        banks = {}
+        for m in range(MB):
+            for j in range(PIECES):
+                banks[m, j] = psum.tile([P, PIECE], F32, name=f"bank{m}{j}")
+        for k in range(KB):
+            for m in range(MB):
+                for j in range(PIECES):
+                    picked = blocks[k][:].indirect(offsets[:, j * OFFS_COLS : (j + 1) * OFFS_COLS])
+                    nc.tensor.matmul(
+                        banks[m, j][:],
+                        weights[:, k, m * P : (m + 1) * P],
+                        picked,
+                        start=k == 0,
+                        stop=k == KB - 1,
+                    )
+
+        for m in range(MB):
+            pooled = held.tile([P, PIECES * GROUPS], F32, name=f"pooled{m}")
+            for j in range(PIECES):
+                z = held.tile([P, PIECE], F32, name=f"z{m}{j}")
+                nc.scalar.activation(z[:], banks[m, j][:], SILU, bias=bias[:, m : m + 1])
+                sums = held.tile([P, GROUPS], F32, name=f"sums{m}{j}")
+                nc.vector.tensor_reduce(sums[:], z[:].rearrange("p (v t) -> p v t", t=D), AXIS_X, ADD)
+                nc.vector.tensor_scalar(
+                    pooled[:, j * GROUPS : (j + 1) * GROUPS], sums[:], 1.0 / D, None, MULT
+                )
+            nc.sync.dma_start(out[m * P : (m + 1) * P, :], pooled[:])

@@ -23,15 +23,13 @@ def tile_gather_matmul_kernel(tc, table, w, b, offs, out):
         tc.psum_pool(name="psum", bufs=1) as psum,
     ):
         offsets = held.tile([P, N // 16], U16, name="offsets")
-        nc.sync.dma_start(offsets[:], offs)
         weights = held.tile([P, KB, M], BF16, name="weights")
-        nc.scalar.dma_start(weights[:], w.rearrange("(a p) m -> p a m", p=P))
-        blocks = []
-        for k in range(KB):
-            block = held.tile([P, S], BF16, name=f"block{k}")
-            nc.sync.dma_start(block[:], table[k * P : (k + 1) * P, :])
-            blocks.append(block)
         bias = held.tile([P, MB], F32, name="bias")
+        blocks = [held.tile([P, S], BF16, name=f"block{k}") for k in range(KB)]
+        nc.sync.dma_start(blocks[0][:], table[0:P, :])
+        nc.sync.dma_start(offsets[:], offs)
+        nc.scalar.dma_start(weights[:], w.rearrange("(a p) m -> p a m", p=P))
+        nc.sync.dma_start(blocks[1][:], table[P:K, :])
         nc.scalar.dma_start(bias[:], b.rearrange("(a p) o -> p (a o)", p=P))
 
         banks = {}

@@ -11,7 +11,7 @@ D = 8
 PIECE = 512
 KB, MB, PIECES = K // P, M // P, N // PIECE
 OFFS_COLS = PIECE // 16
-GROUPS = PIECE // D
+PARTS = 2
 
 FLOPS = 2 * K * M * N
 
@@ -48,14 +48,21 @@ def tile_gather_matmul_kernel(tc, table, w, b, offs, out):
                         stop=k == KB - 1,
                     )
 
+        part = PIECE // PARTS
         for m in range(MB):
-            pooled = held.tile([P, PIECES * GROUPS], F32, name=f"pooled{m}")
+            sums = held.tile([P, N // D], F32, name=f"sums{m}")
             for j in range(PIECES):
                 z = held.tile([P, PIECE], F32, name=f"z{m}{j}")
-                nc.scalar.activation(z[:], banks[m, j][:], SILU, bias=bias[:, m : m + 1])
-                sums = held.tile([P, GROUPS], F32, name=f"sums{m}{j}")
-                nc.vector.tensor_reduce(sums[:], z[:].rearrange("p (v t) -> p v t", t=D), AXIS_X, ADD)
-                nc.vector.tensor_scalar(
-                    pooled[:, j * GROUPS : (j + 1) * GROUPS], sums[:], 1.0 / D, None, MULT
-                )
+                for c in range(PARTS):
+                    cols = slice(c * part, (c + 1) * part)
+                    nc.scalar.activation(z[:, cols], banks[m, j][:, cols], SILU, bias=bias[:, m : m + 1])
+                    first = (j * PIECE + c * part) // D
+                    nc.vector.tensor_reduce(
+                        sums[:, first : first + part // D],
+                        z[:, cols].rearrange("p (v t) -> p v t", t=D),
+                        AXIS_X,
+                        ADD,
+                    )
+            pooled = held.tile([P, N // D], F32, name=f"pooled{m}")
+            nc.vector.tensor_scalar(pooled[:], sums[:], 1.0 / D, None, MULT)
             nc.sync.dma_start(out[m * P : (m + 1) * P, :], pooled[:])

import concourse.mybir as mybir

BF16, F32, U16 = mybir.dt.bfloat16, mybir.dt.float32, mybir.dt.uint16
SILU = mybir.ActivationFunctionType.Silu
ADD, MULT = mybir.AluOpType.add, mybir.AluOpType.mult
AXIS_X = mybir.AxisListType.X

P = 128
S, K, M, N = 4096, 256, 256, 1024
D = 8
PIECE = 512
KB, MB, PIECES = K // P, M // P, N // PIECE
OFFS_COLS = PIECE // 16
PARTS = 2

FLOPS = 2 * K * M * N


def tile_gather_matmul_kernel(tc, table, w, b, offs, out):
    nc = tc.nc
    with (
        tc.tile_pool(name="held", bufs=1) as held,
        tc.psum_pool(name="psum", bufs=1) as psum,
    ):
        offsets = held.tile([P, N // 16], U16, name="offsets")
        weights = held.tile([P, KB, M], BF16, name="weights")
        bias = held.tile([P, MB], F32, name="bias")
        blocks = [held.tile([P, S], BF16, name=f"block{k}") for k in range(KB)]
        nc.sync.dma_start(blocks[0][:], table[0:P, :])
        nc.sync.dma_start(offsets[:], offs)
        nc.scalar.dma_start(weights[:], w.rearrange("(a p) m -> p a m", p=P))
        nc.sync.dma_start(blocks[1][:], table[P:K, :])
        nc.scalar.dma_start(bias[:], b.rearrange("(a p) o -> p (a o)", p=P))

        banks = {}
        for m in range(MB):
            for j in range(PIECES):
                banks[m, j] = psum.tile([P, PIECE], F32, name=f"bank{m}{j}")
        for k in range(KB):
            for m in range(MB):
                for j in range(PIECES):
                    picked = blocks[k][:].indirect(offsets[:, j * OFFS_COLS : (j + 1) * OFFS_COLS])
                    nc.tensor.matmul(
                        banks[m, j][:],
                        weights[:, k, m * P : (m + 1) * P],
                        picked,
                        start=k == 0,
                        stop=k == KB - 1,
                    )

        part = PIECE // PARTS
        for m in range(MB):
            sums = held.tile([P, N // D], F32, name=f"sums{m}")
            for j in range(PIECES):
                z = held.tile([P, PIECE], F32, name=f"z{m}{j}")
                for c in range(PARTS):
                    cols = slice(c * part, (c + 1) * part)
                    nc.scalar.activation(z[:, cols], banks[m, j][:, cols], SILU, bias=bias[:, m : m + 1])
                    first = (j * PIECE + c * part) // D
                    nc.vector.tensor_reduce(
                        sums[:, first : first + part // D],
                        z[:, cols].rearrange("p (v t) -> p v t", t=D),
                        AXIS_X,
                        ADD,
                    )
            pooled = held.tile([P, N // D], F32, name=f"pooled{m}")
            nc.vector.tensor_scalar(pooled[:], sums[:], 1.0 / D, None, MULT)
            nc.sync.dma_start(out[m * P : (m + 1) * P, :], pooled[:])
